import numpy as np
import ml_dtypes


def mxq(x, axis, fmt="e4m3"):
    dtype, down = {"e4m3": (ml_dtypes.float8_e4m3fn, 7), "e5m2": (ml_dtypes.float8_e5m2, 14)}[fmt]
    v = np.moveaxis(np.asarray(x, np.float32).astype(ml_dtypes.bfloat16).astype(np.float64), axis, -1)
    blocks = v.reshape(v.shape[:-1] + (-1, 32))
    amax = np.abs(blocks).max(-1, keepdims=True)
    byte = np.maximum(np.where(amax > 0, np.frexp(amax)[1] - 1 + 127, 0) - down, 1)
    scale = np.exp2(byte - 127.0)
    codes = (blocks / scale).astype(np.float32).astype(dtype).astype(np.float64)
    return np.moveaxis((codes * scale).reshape(v.shape), -1, axis)


WIDE = False


def mx_kscale(k):
    if not WIDE:
        return np.ones(k)
    levels = np.array([10, -10, 5, -5, 0])
    if k % 512:
        return np.exp2(np.random.permutation(np.resize(levels, k // 32))).repeat(32)
    a = np.empty((k // 512, 16))
    for p in range(k // 512):
        a[p, :8] = np.random.permutation(np.resize(levels, 8))
        for g in range(8):
            far = levels[np.abs(levels - a[p, g]) >= 10]
            a[p, g + 8] = far[np.random.randint(len(far))]
    return np.exp2(a.ravel()).repeat(32)


def f64(x):
    return np.asarray(x).astype(np.float64)


def striped(idx):
    return np.tile(idx.reshape(-1, 16).T, (8, 1)).astype(np.uint16)


def unstriped(offs):
    return offs[:16].T.reshape(-1).astype(np.int64)


def pack_weight(w):
    k, n = w.shape
    w = f64(np.asarray(w, np.float32).astype(ml_dtypes.bfloat16)).reshape(k // 32, 32, n)
    amax = np.abs(w).max(1)
    byte = np.clip(np.where(amax > 0, np.frexp(amax)[1] - 1 + 127 - 7, 1), 1, 254)
    scaled = (w * np.exp2(127.0 - byte)[:, None, :]).reshape(k, n).astype(np.float32)
    words = np.ascontiguousarray(scaled.reshape(k // 512, 128, 4, n).transpose(0, 1, 3, 2)).astype(ml_dtypes.float8_e4m3fn).view(np.uint8)
    return words, np.ascontiguousarray(byte.astype(np.uint8).reshape(k // 512, 16, n))


def unpack_weight(words, scales):
    g, p, n, _ = words.shape
    vals = np.ascontiguousarray(words).view(ml_dtypes.float8_e4m3fn).astype(np.float64) * np.repeat(np.exp2(scales.astype(np.float64) - 127.0), 8, axis=1)[..., None]
    return vals.transpose(0, 1, 3, 2).reshape(g * 512, n)


K, T, S, N, U = 1024, 1024, 512, 128, 512


def setup_inputs():
    n = np.random.standard_normal
    s = mx_kscale(K)[:, None]
    packed_xT = pack_weight(n((K, T)) * s)
    return {
        "x_words": packed_xT[0],
        "x_scales": packed_xT[1],
        "w1": (n((K, N)) / np.sqrt(K) / s).astype(np.float32),
        "w2": (n((K, N)) / np.sqrt(K) / s).astype(np.float32),
        "offs": striped(np.random.permutation(T)[:S]),
        "lc": striped(np.random.randint(0, S, U)),
        "rc": striped(np.random.randint(0, S, U)),
    }


def reference(x_words, x_scales, w1, w2, offs, lc, rc):
    xq = unpack_weight(x_words, x_scales)[:, unstriped(offs)]
    y = mxq(f64(w1), 0, "e4m3").T @ xq
    ul = y[:, unstriped(lc)]
    z = mxq(f64(w2), 0, "e4m3").T @ xq
    snd = np.log(np.exp(z) + 1.0) + 0.3
    al = snd[:, unstriped(lc)]
    ur = y[:, unstriped(rc)]
    ar = snd[:, unstriped(rc)]
    sr = np.maximum(np.maximum(ul + al, ur + ar), 0.01 * ar)
    sl = np.minimum(np.minimum(ul - al, ur - ar), -0.01 * al)
    wd = sr - sl
    return (0.5 * (sr * ((ul) ** 2) - (sl * ((ur) ** 2))) + (sl * sr) * (ur - ul)) / wd

@@ -1,0 +1,176 @@
+import math
+from contextlib import ExitStack
+
+import concourse.mybir as mybir
+
+K, T, S, N, U = 1024, 1024, 512, 128, 512
+FLOPS = 2 * 2 * K * N * S
+
+F32 = mybir.dt.float32
+BF16 = mybir.dt.bfloat16
+I32 = mybir.dt.int32
+U32 = mybir.dt.uint32
+U16 = mybir.dt.uint16
+U8 = mybir.dt.uint8
+FP8X4 = mybir.dt.float8_e4m3fn_x4
+ALU = mybir.AluOpType
+ACT = mybir.ActivationFunctionType
+
+P = 128
+PACK = 4
+K_PASS = P * PACK
+PASSES = K // K_PASS
+VECTOR_WINDOW = 704
+SCALAR_WINDOW = 2048
+HALF = U // 2
+
+
+def tile_picked_yhllf_face_p_kernel(tc, x_words, x_scales, w1, w2, offs, lc, rc, out):
+    nc = tc.nc
+    with ExitStack() as ctx:
+        keep = ctx.enter_context(tc.tile_pool(name="keep", bufs=1))
+        psum = ctx.enter_context(tc.psum_pool(name="psum", bufs=1))
+        halves = [slice(h * HALF, (h + 1) * HALF) for h in range(2)]
+
+        offs_sb = keep.tile([P, S // 16], U16, name="offs_sb")
+        lc_sb = keep.tile([P, U // 16], U16, name="lc_sb")
+        rc_sb = keep.tile([P, U // 16], U16, name="rc_sb")
+
+        all_scales = keep.tile([P, T], U8, name="all_scales", align_bytes=64)
+        nc.vector.memset(all_scales[:].bitcast(I32), 0)
+        nc.sync.dma_start(offs_sb[:], offs)
+        for q, queue in enumerate((nc.sync, nc.scalar, nc.sync, nc.scalar)):
+            queue.dma_start(
+                out=all_scales[32 * q : 32 * q + 4 * PASSES, :].bitcast(I32),
+                in_=x_scales[:, 4 * q : 4 * q + 4, :].bitcast(I32),
+            )
+
+        all_words = [keep.tile([P, T], I32, name="all_words%d" % g, align_bytes=64) for g in range(PASSES)]
+        raw = {}
+
+        def load_words(g):
+            nc.sync.dma_start(out=all_words[g][:], in_=x_words[g].rearrange("p n t -> p (n t)").bitcast(I32))
+
+        def load_weight(label, w, g):
+            raw[label, g] = keep.tile([P, PACK, N], F32, name="raw_%s%d" % (label, g))
+            nc.sync.dma_start(
+                out=raw[label, g][:],
+                in_=w[g * K_PASS : (g + 1) * K_PASS, :].rearrange("(p j) n -> p j n", j=PACK),
+            )
+
+        load_words(0)
+        load_weight("w2", w2, 0)
+        load_weight("w1", w1, 0)
+        load_weight("w2", w2, 1)
+        load_words(1)
+        load_weight("w1", w1, 1)
+        nc.sync.dma_start(lc_sb[:], lc)
+        nc.sync.dma_start(rc_sb[:], rc)
+
+        state = keep.tile([P, VECTOR_WINDOW], F32, name="state")
+        speed = keep.tile([P, VECTOR_WINDOW], F32, name="speed")
+        log_speed = keep.tile([P, SCALAR_WINDOW], F32, name="log_speed")
+        nc.vector.memset(state[:, S:], 0.0)
+        nc.vector.memset(speed[:, S:], 0.0)
+
+        picked_scales = keep.tile([P, S], U8, name="picked_scales", align_bytes=64)
+        picked_words = [keep.tile([P, S], U32, name="picked_words%d" % g, align_bytes=64) for g in range(PASSES)]
+        nc.vector.tensor_copy(picked_scales[:], all_scales[:].indirect(offs_sb[:]))
+
+        codes, scales = {}, {}
+
+        def quantise_weight(label, g):
+            grouped = keep.tile([P, N, PACK], BF16, name="grouped_%s%d" % (label, g), align_bytes=64)
+            nc.scalar.copy(out=grouped[:], in_=raw[label, g][:].rearrange("p j n -> p n j"))
+            codes[label, g] = keep.tile([P, N], U32, name="codes_%s%d" % (label, g), align_bytes=64)
+            scales[label, g] = keep.tile([P, N], U8, name="scales_%s%d" % (label, g), align_bytes=64)
+            nc.vector.quantize_mx(
+                out=codes[label, g][:].bitcast(FP8X4),
+                scales=scales[label, g][:],
+                in_=grouped[:].rearrange("p n j -> p (n j)"),
+            )
+
+        banks = {(label, h): psum.tile([P, HALF], F32, name="bank_%s%d" % (label, h)) for label in ("w2", "w1") for h in range(2)}
+
+        def multiply(label, g):
+            for h, cols in enumerate(halves):
+                nc.tensor.matmul_mx(
+                    out=banks[label, h][:],
+                    lhsT=codes[label, g][:].bitcast(FP8X4),
+                    lhsT_scale=scales[label, g][:],
+                    rhs=picked_words[g][:, cols].bitcast(FP8X4),
+                    rhs_scale=picked_scales[4 * g : P, cols],
+                    start=(g == 0),
+                    stop=(g == PASSES - 1),
+                )
+
+        nc.vector.tensor_copy(picked_words[0][:], all_words[0][:].bitcast(U32).indirect(offs_sb[:]))
+        quantise_weight("w2", 0)
+        multiply("w2", 0)
+        quantise_weight("w1", 0)
+        multiply("w1", 0)
+        quantise_weight("w2", 1)
+        for h, cols in enumerate(halves):
+            nc.vector.tensor_copy(
+                picked_words[1][:, cols], all_words[1][:].bitcast(U32).indirect(offs_sb[:, 16 * h : 16 * (h + 1)])
+            )
+        multiply("w2", 1)
+        quantise_weight("w1", 1)
+        multiply("w1", 1)
+
+        def face(name):
+            return keep.tile([P, U], F32, name=name)
+
+        abs_z, decay, fl = (log_speed[:, i * S : (i + 1) * S] for i in (1, 2, 3))
+        log_term = keep.tile([P, S], F32, name="log_term", tag="shared")
+        for h, cols in enumerate(halves):
+            nc.scalar.activation(abs_z[:, cols], banks["w2", h][:], ACT.Abs)
+            nc.scalar.activation(decay[:, cols], abs_z[:, cols], ACT.Exp, scale=-1.0)
+        floor = math.exp(0.3)
+        nc.scalar.activation(log_term[:], decay, ACT.Ln, scale=floor, bias=floor)
+
+        for h, cols in enumerate(halves):
+            nc.vector.tensor_copy(state[:, cols], banks["w1", h][:])
+        ul, ur, al, ar = face("ul"), face("ur"), face("al"), face("ar")
+        nc.vector.tensor_copy(ul[:], state[:].indirect(lc_sb[:]))
+        nc.vector.tensor_copy(ur[:], state[:].indirect(rc_sb[:]))
+
+        nc.scalar.activation(fl, ul[:], ACT.Square, scale=math.sqrt(0.5))
+        for h, cols in enumerate(halves):
+            nc.vector.scalar_tensor_tensor(speed[:, cols], banks["w2", h][:], 0.0, log_term[:, cols], ALU.max, ALU.add)
+            nc.scalar.activation(log_speed[:, cols], speed[:, cols], ACT.Ln)
+        nc.scalar.activation(al[:], log_speed[:].indirect(lc_sb[:]), ACT.Exp)
+        nc.vector.tensor_copy(ar[:], speed[:].indirect(rc_sb[:]))
+
+        pair = keep.tile([P, 2 * U], F32, name="pair", tag="shared")
+        total, drop = pair[:, :U], pair[:, U:]
+        nc.vector.tensor_tensor(total, ul[:], ur[:], ALU.add)
+        nc.vector.tensor_tensor(drop, ul[:], ur[:], ALU.subtract)
+
+        pr, nr, pl, nl = face("pr"), face("nr"), face("pl"), face("nl")
+        prc, nlc, sr, ns = face("prc"), face("nlc"), face("sr"), face("ns")
+        nc.vector.tensor_tensor(pr[:], ar[:], ur[:], ALU.add)
+        nc.vector.tensor_tensor(nr[:], ar[:], ur[:], ALU.subtract)
+        nc.vector.scalar_tensor_tensor(prc[:], ar[:], 0.01, pr[:], ALU.mult, ALU.max)
+        nc.vector.tensor_tensor(nl[:], al[:], ul[:], ALU.subtract)
+        nc.vector.tensor_tensor(pl[:], al[:], ul[:], ALU.add)
+        nc.vector.scalar_tensor_tensor(nlc[:], al[:], 0.01, nl[:], ALU.mult, ALU.max)
+        nc.vector.tensor_tensor(sr[:], pl[:], prc[:], ALU.max)
+        nc.vector.tensor_tensor(ns[:], nlc[:], nr[:], ALU.max)
+
+        t, wd, root, rw = face("t"), face("wd"), face("root"), face("rw")
+        q1, q2, q3, flux = face("q1"), face("q2"), face("q3"), face("flux")
+        nc.vector.scalar_tensor_tensor(t[:], total, -0.5, sr[:], ALU.mult, ALU.add)
+        for h in halves:
+            nc.vector.tensor_tensor(wd[:, h], sr[:, h], ns[:, h], ALU.add)
+            nc.scalar.activation(root[:, h], wd[:, h], ACT.Abs_reciprocal_sqrt)
+            nc.scalar.activation(rw[:, h], root[:, h], ACT.Square)
+        for h in halves:
+            nc.vector.tensor_tensor(q1[:, h], ns[:, h], drop[:, h], ALU.mult)
+        for h in halves:
+            nc.vector.tensor_tensor(q2[:, h], q1[:, h], t[:, h], ALU.mult)
+        for h in halves:
+            nc.vector.tensor_tensor(q3[:, h], q2[:, h], rw[:, h], ALU.mult)
+        for h, queue in zip(halves, (nc.sync, nc.scalar)):
+            nc.vector.tensor_tensor(flux[:, h], q3[:, h], fl[:, h], ALU.add)
+            queue.dma_start(out=out[:, h], in_=flux[:, h])

@@ -39,13 +39,8 @@ def tile_picked_yhllf_face_p_kernel(tc, x_words, x_scales, w1, w2, offs, lc, rc,
         all_scales = keep.tile([P, T], U8, name="all_scales", align_bytes=64)
         nc.vector.memset(all_scales[:].bitcast(I32), 0)
         nc.sync.dma_start(offs_sb[:], offs)
-        for q, queue in enumerate((nc.sync, nc.scalar, nc.sync, nc.scalar)):
-            queue.dma_start(
-                out=all_scales[32 * q : 32 * q + 4 * PASSES, :].bitcast(I32),
-                in_=x_scales[:, 4 * q : 4 * q + 4, :].bitcast(I32),
-            )
 
-        all_words = [keep.tile([P, T], I32, name="all_words%d" % g, align_bytes=64) for g in range(PASSES)]
+        all_words = [keep.tile([P, T], I32, name="all_words%d" % g, tag="words%d" % g, align_bytes=64) for g in range(PASSES)]
         raw = {}
 
         def load_words(g):
@@ -59,36 +54,46 @@ def tile_picked_yhllf_face_p_kernel(tc, x_words, x_scales, w1, w2, offs, lc, rc,
             )
 
         load_words(0)
-        load_weight("w2", w2, 0)
+        for q, queue in enumerate((nc.sync, nc.scalar, nc.sync, nc.scalar)):
+            queue.dma_start(
+                out=all_scales[32 * q : 32 * q + 4 * PASSES, :].bitcast(I32),
+                in_=x_scales[:, 4 * q : 4 * q + 4, :].bitcast(I32),
+            )
         load_weight("w1", w1, 0)
-        load_weight("w2", w2, 1)
-        load_words(1)
+        load_weight("w2", w2, 0)
         load_weight("w1", w1, 1)
+        load_words(1)
+        load_weight("w2", w2, 1)
         nc.sync.dma_start(lc_sb[:], lc)
         nc.sync.dma_start(rc_sb[:], rc)
 
-        state = keep.tile([P, VECTOR_WINDOW], F32, name="state")
-        speed = keep.tile([P, VECTOR_WINDOW], F32, name="speed")
-        log_speed = keep.tile([P, SCALAR_WINDOW], F32, name="log_speed")
-        nc.vector.memset(state[:, S:], 0.0)
+        speed = keep.tile([P, VECTOR_WINDOW], F32, name="speed", tag="speed")
+        log_speed = keep.tile([P, SCALAR_WINDOW], F32, name="log_speed", tag="window")
         nc.vector.memset(speed[:, S:], 0.0)
+        nc.vector.memset(log_speed[:, 3 * S :], 0.0)
+        warm = keep.tile([P, 8], F32, name="warm")
+        nc.scalar.activation(warm[:], speed[:, S : S + 8], ACT.Sigmoid)
 
         picked_scales = keep.tile([P, S], U8, name="picked_scales", align_bytes=64)
-        picked_words = [keep.tile([P, S], U32, name="picked_words%d" % g, align_bytes=64) for g in range(PASSES)]
-        nc.vector.tensor_copy(picked_scales[:], all_scales[:].indirect(offs_sb[:]))
+        picked_words = {}
 
         codes, scales = {}, {}
 
-        def quantise_weight(label, g):
-            grouped = keep.tile([P, N, PACK], BF16, name="grouped_%s%d" % (label, g), align_bytes=64)
-            nc.scalar.copy(out=grouped[:], in_=raw[label, g][:].rearrange("p j n -> p n j"))
-            codes[label, g] = keep.tile([P, N], U32, name="codes_%s%d" % (label, g), align_bytes=64)
-            scales[label, g] = keep.tile([P, N], U8, name="scales_%s%d" % (label, g), align_bytes=64)
+        def quantise(parts, slot_in, slot_out):
+            count = len(parts)
+            grouped = keep.tile([P, count, N, PACK], BF16, name=slot_in, tag=slot_in, align_bytes=64)
+            for i, part in enumerate(parts):
+                nc.scalar.copy(out=grouped[:, i], in_=raw[part][:].rearrange("p j n -> p n j"))
+            words = keep.tile([P, count * N], U32, name="codes_" + slot_in, tag=slot_out, align_bytes=64)
+            plane = keep.tile([P, count * N], U8, name="scales_" + slot_in, align_bytes=64)
             nc.vector.quantize_mx(
-                out=codes[label, g][:].bitcast(FP8X4),
-                scales=scales[label, g][:],
-                in_=grouped[:].rearrange("p n j -> p (n j)"),
+                out=words[:].bitcast(FP8X4),
+                scales=plane[:],
+                in_=grouped[:].rearrange("p i n j -> p (i n j)"),
             )
+            for i, part in enumerate(parts):
+                codes[part] = words[:, i * N : (i + 1) * N]
+                scales[part] = plane[:, i * N : (i + 1) * N]
 
         banks = {(label, h): psum.tile([P, HALF], F32, name="bank_%s%d" % (label, h)) for label in ("w2", "w1") for h in range(2)}
 
@@ -96,66 +101,69 @@ def tile_picked_yhllf_face_p_kernel(tc, x_words, x_scales, w1, w2, offs, lc, rc,
             for h, cols in enumerate(halves):
                 nc.tensor.matmul_mx(
                     out=banks[label, h][:],
-                    lhsT=codes[label, g][:].bitcast(FP8X4),
-                    lhsT_scale=scales[label, g][:],
+                    lhsT=codes[label, g].bitcast(FP8X4),
+                    lhsT_scale=scales[label, g],
                     rhs=picked_words[g][:, cols].bitcast(FP8X4),
                     rhs_scale=picked_scales[4 * g : P, cols],
                     start=(g == 0),
                     stop=(g == PASSES - 1),
                 )
 
+        picked_words[0] = keep.tile([P, S], U32, name="picked_words0", align_bytes=64)
         nc.vector.tensor_copy(picked_words[0][:], all_words[0][:].bitcast(U32).indirect(offs_sb[:]))
-        quantise_weight("w2", 0)
-        multiply("w2", 0)
-        quantise_weight("w1", 0)
+        nc.vector.tensor_copy(picked_scales[:], all_scales[:].indirect(offs_sb[:]))
+        quantise([("w1", 0), ("w2", 0)], "first_pass", "first_codes")
         multiply("w1", 0)
-        quantise_weight("w2", 1)
+        multiply("w2", 0)
+        quantise([("w1", 1)], "state_tail", "state_codes")
+        picked_words[1] = keep.tile([P, S], U32, name="picked_words1", tag="state_tail", align_bytes=64)
         for h, cols in enumerate(halves):
             nc.vector.tensor_copy(
                 picked_words[1][:, cols], all_words[1][:].bitcast(U32).indirect(offs_sb[:, 16 * h : 16 * (h + 1)])
             )
-        multiply("w2", 1)
-        quantise_weight("w1", 1)
         multiply("w1", 1)
+        quantise([("w2", 1)], "speed_tail", "words1")
+        multiply("w2", 1)
 
         def face(name):
             return keep.tile([P, U], F32, name=name)
 
-        abs_z, decay, fl = (log_speed[:, i * S : (i + 1) * S] for i in (1, 2, 3))
-        log_term = keep.tile([P, S], F32, name="log_term", tag="shared")
+        tail, log_tail = (log_speed[:, i * S : (i + 1) * S] for i in (1, 2))
         for h, cols in enumerate(halves):
-            nc.scalar.activation(abs_z[:, cols], banks["w2", h][:], ACT.Abs)
-            nc.scalar.activation(decay[:, cols], abs_z[:, cols], ACT.Exp, scale=-1.0)
-        floor = math.exp(0.3)
-        nc.scalar.activation(log_term[:], decay, ACT.Ln, scale=floor, bias=floor)
+            nc.scalar.activation(tail[:, cols], banks["w2", h][:], ACT.Sigmoid, scale=-1.0)
+        for cols in halves:
+            nc.scalar.activation(log_tail[:, cols], tail[:, cols], ACT.Ln, bias=2.0**-60)
 
+        state = keep.tile([P, S], F32, name="state", tag="speed_tail", align_bytes=64)
         for h, cols in enumerate(halves):
             nc.vector.tensor_copy(state[:, cols], banks["w1", h][:])
         ul, ur, al, ar = face("ul"), face("ur"), face("al"), face("ar")
-        nc.vector.tensor_copy(ul[:], state[:].indirect(lc_sb[:]))
-        nc.vector.tensor_copy(ur[:], state[:].indirect(rc_sb[:]))
+        for picked, cells in ((ul, lc_sb), (ur, rc_sb)):
+            for h, cols in enumerate(halves):
+                nc.vector.tensor_copy(picked[:, cols], state[:].indirect(cells[:, 16 * h : 16 * (h + 1)]))
 
-        nc.scalar.activation(fl, ul[:], ACT.Square, scale=math.sqrt(0.5))
         for h, cols in enumerate(halves):
-            nc.vector.scalar_tensor_tensor(speed[:, cols], banks["w2", h][:], 0.0, log_term[:, cols], ALU.max, ALU.add)
-            nc.scalar.activation(log_speed[:, cols], speed[:, cols], ACT.Ln)
+            nc.vector.scalar_tensor_tensor(speed[:, cols], log_tail[:, cols], -1.0, banks["w2", h][:], ALU.mult, ALU.max)
+            nc.scalar.activation(log_speed[:, cols], speed[:, cols], ACT.Ln, bias=0.3)
         nc.scalar.activation(al[:], log_speed[:].indirect(lc_sb[:]), ACT.Exp)
         nc.vector.tensor_copy(ar[:], speed[:].indirect(rc_sb[:]))
 
-        pair = keep.tile([P, 2 * U], F32, name="pair", tag="shared")
+        fl = keep.tile([P, U], F32, name="fl", tag="window")
+        nc.scalar.activation(fl[:], ul[:], ACT.Square, scale=math.sqrt(0.5))
+        pair = keep.tile([P, 2 * U], F32, name="pair", tag="speed")
         total, drop = pair[:, :U], pair[:, U:]
-        nc.vector.tensor_tensor(total, ul[:], ur[:], ALU.add)
-        nc.vector.tensor_tensor(drop, ul[:], ur[:], ALU.subtract)
 
         pr, nr, pl, nl = face("pr"), face("nr"), face("pl"), face("nl")
         prc, nlc, sr, ns = face("prc"), face("nlc"), face("sr"), face("ns")
-        nc.vector.tensor_tensor(pr[:], ar[:], ur[:], ALU.add)
-        nc.vector.tensor_tensor(nr[:], ar[:], ur[:], ALU.subtract)
+        nc.vector.scalar_tensor_tensor(pr[:], ar[:], 0.99 * 0.3, ur[:], ALU.add, ALU.add)
+        nc.vector.scalar_tensor_tensor(nr[:], ar[:], 0.3, ur[:], ALU.add, ALU.subtract)
+        nc.vector.tensor_tensor(total, ul[:], ur[:], ALU.add)
+        nc.vector.tensor_tensor(drop, ul[:], ur[:], ALU.subtract)
         nc.vector.scalar_tensor_tensor(prc[:], ar[:], 0.01, pr[:], ALU.mult, ALU.max)
         nc.vector.tensor_tensor(nl[:], al[:], ul[:], ALU.subtract)
         nc.vector.tensor_tensor(pl[:], al[:], ul[:], ALU.add)
         nc.vector.scalar_tensor_tensor(nlc[:], al[:], 0.01, nl[:], ALU.mult, ALU.max)
-        nc.vector.tensor_tensor(sr[:], pl[:], prc[:], ALU.max)
+        nc.vector.scalar_tensor_tensor(sr[:], prc[:], 0.01 * 0.3, pl[:], ALU.add, ALU.max)
         nc.vector.tensor_tensor(ns[:], nlc[:], nr[:], ALU.max)
 
         t, wd, root, rw = face("t"), face("wd"), face("root"), face("rw")

import math
from contextlib import ExitStack

import concourse.mybir as mybir

K, T, S, N, U = 1024, 1024, 512, 128, 512
FLOPS = 2 * 2 * K * N * S

F32 = mybir.dt.float32
BF16 = mybir.dt.bfloat16
I32 = mybir.dt.int32
U32 = mybir.dt.uint32
U16 = mybir.dt.uint16
U8 = mybir.dt.uint8
FP8X4 = mybir.dt.float8_e4m3fn_x4
ALU = mybir.AluOpType
ACT = mybir.ActivationFunctionType

P = 128
PACK = 4
K_PASS = P * PACK
PASSES = K // K_PASS
VECTOR_WINDOW = 704
SCALAR_WINDOW = 2048
HALF = U // 2


def tile_picked_yhllf_face_p_kernel(tc, x_words, x_scales, w1, w2, offs, lc, rc, out):
    nc = tc.nc
    with ExitStack() as ctx:
        keep = ctx.enter_context(tc.tile_pool(name="keep", bufs=1))
        psum = ctx.enter_context(tc.psum_pool(name="psum", bufs=1))
        halves = [slice(h * HALF, (h + 1) * HALF) for h in range(2)]

        offs_sb = keep.tile([P, S // 16], U16, name="offs_sb")
        lc_sb = keep.tile([P, U // 16], U16, name="lc_sb")
        rc_sb = keep.tile([P, U // 16], U16, name="rc_sb")

        all_scales = keep.tile([P, T], U8, name="all_scales", align_bytes=64)
        nc.vector.memset(all_scales[:].bitcast(I32), 0)
        nc.sync.dma_start(offs_sb[:], offs)

        all_words = [keep.tile([P, T], I32, name="all_words%d" % g, tag="words%d" % g, align_bytes=64) for g in range(PASSES)]
        raw = {}

        def load_words(g):
            nc.sync.dma_start(out=all_words[g][:], in_=x_words[g].rearrange("p n t -> p (n t)").bitcast(I32))

        def load_weight(label, w, g):
            raw[label, g] = keep.tile([P, PACK, N], F32, name="raw_%s%d" % (label, g))
            nc.sync.dma_start(
                out=raw[label, g][:],
                in_=w[g * K_PASS : (g + 1) * K_PASS, :].rearrange("(p j) n -> p j n", j=PACK),
            )

        load_words(0)
        for q, queue in enumerate((nc.sync, nc.scalar, nc.sync, nc.scalar)):
            queue.dma_start(
                out=all_scales[32 * q : 32 * q + 4 * PASSES, :].bitcast(I32),
                in_=x_scales[:, 4 * q : 4 * q + 4, :].bitcast(I32),
            )
        load_weight("w1", w1, 0)
        load_weight("w2", w2, 0)
        load_weight("w1", w1, 1)
        load_words(1)
        load_weight("w2", w2, 1)
        nc.sync.dma_start(lc_sb[:], lc)
        nc.sync.dma_start(rc_sb[:], rc)

        speed = keep.tile([P, VECTOR_WINDOW], F32, name="speed", tag="speed")
        log_speed = keep.tile([P, SCALAR_WINDOW], F32, name="log_speed", tag="window")
        nc.vector.memset(speed[:, S:], 0.0)
        nc.vector.memset(log_speed[:, 3 * S :], 0.0)
        warm = keep.tile([P, 8], F32, name="warm")
        nc.scalar.activation(warm[:], speed[:, S : S + 8], ACT.Sigmoid)

        picked_scales = keep.tile([P, S], U8, name="picked_scales", align_bytes=64)
        picked_words = {}

        codes, scales = {}, {}

        def quantise(parts, slot_in, slot_out):
            count = len(parts)
            grouped = keep.tile([P, count, N, PACK], BF16, name=slot_in, tag=slot_in, align_bytes=64)
            for i, part in enumerate(parts):
                nc.scalar.copy(out=grouped[:, i], in_=raw[part][:].rearrange("p j n -> p n j"))
            words = keep.tile([P, count * N], U32, name="codes_" + slot_in, tag=slot_out, align_bytes=64)
            plane = keep.tile([P, count * N], U8, name="scales_" + slot_in, align_bytes=64)
            nc.vector.quantize_mx(
                out=words[:].bitcast(FP8X4),
                scales=plane[:],
                in_=grouped[:].rearrange("p i n j -> p (i n j)"),
            )
            for i, part in enumerate(parts):
                codes[part] = words[:, i * N : (i + 1) * N]
                scales[part] = plane[:, i * N : (i + 1) * N]

        banks = {(label, h): psum.tile([P, HALF], F32, name="bank_%s%d" % (label, h)) for label in ("w2", "w1") for h in range(2)}

        def multiply(label, g):
            for h, cols in enumerate(halves):
                nc.tensor.matmul_mx(
                    out=banks[label, h][:],
                    lhsT=codes[label, g].bitcast(FP8X4),
                    lhsT_scale=scales[label, g],
                    rhs=picked_words[g][:, cols].bitcast(FP8X4),
                    rhs_scale=picked_scales[4 * g : P, cols],
                    start=(g == 0),
                    stop=(g == PASSES - 1),
                )

        picked_words[0] = keep.tile([P, S], U32, name="picked_words0", align_bytes=64)
        nc.vector.tensor_copy(picked_words[0][:], all_words[0][:].bitcast(U32).indirect(offs_sb[:]))
        nc.vector.tensor_copy(picked_scales[:], all_scales[:].indirect(offs_sb[:]))
        quantise([("w1", 0), ("w2", 0)], "first_pass", "first_codes")
        multiply("w1", 0)
        multiply("w2", 0)
        quantise([("w1", 1)], "state_tail", "state_codes")
        picked_words[1] = keep.tile([P, S], U32, name="picked_words1", tag="state_tail", align_bytes=64)
        for h, cols in enumerate(halves):
            nc.vector.tensor_copy(
                picked_words[1][:, cols], all_words[1][:].bitcast(U32).indirect(offs_sb[:, 16 * h : 16 * (h + 1)])
            )
        multiply("w1", 1)
        quantise([("w2", 1)], "speed_tail", "words1")
        multiply("w2", 1)

        def face(name):
            return keep.tile([P, U], F32, name=name)

        tail, log_tail = (log_speed[:, i * S : (i + 1) * S] for i in (1, 2))
        for h, cols in enumerate(halves):
            nc.scalar.activation(tail[:, cols], banks["w2", h][:], ACT.Sigmoid, scale=-1.0)
        for cols in halves:
            nc.scalar.activation(log_tail[:, cols], tail[:, cols], ACT.Ln, bias=2.0**-60)

        state = keep.tile([P, S], F32, name="state", tag="speed_tail", align_bytes=64)
        for h, cols in enumerate(halves):
            nc.vector.tensor_copy(state[:, cols], banks["w1", h][:])
        ul, ur, al, ar = face("ul"), face("ur"), face("al"), face("ar")
        for picked, cells in ((ul, lc_sb), (ur, rc_sb)):
            for h, cols in enumerate(halves):
                nc.vector.tensor_copy(picked[:, cols], state[:].indirect(cells[:, 16 * h : 16 * (h + 1)]))

        for h, cols in enumerate(halves):
            nc.vector.scalar_tensor_tensor(speed[:, cols], log_tail[:, cols], -1.0, banks["w2", h][:], ALU.mult, ALU.max)
            nc.scalar.activation(log_speed[:, cols], speed[:, cols], ACT.Ln, bias=0.3)
        nc.scalar.activation(al[:], log_speed[:].indirect(lc_sb[:]), ACT.Exp)
        nc.vector.tensor_copy(ar[:], speed[:].indirect(rc_sb[:]))

        fl = keep.tile([P, U], F32, name="fl", tag="window")
        nc.scalar.activation(fl[:], ul[:], ACT.Square, scale=math.sqrt(0.5))
        pair = keep.tile([P, 2 * U], F32, name="pair", tag="speed")
        total, drop = pair[:, :U], pair[:, U:]

        pr, nr, pl, nl = face("pr"), face("nr"), face("pl"), face("nl")
        prc, nlc, sr, ns = face("prc"), face("nlc"), face("sr"), face("ns")
        nc.vector.scalar_tensor_tensor(pr[:], ar[:], 0.99 * 0.3, ur[:], ALU.add, ALU.add)
        nc.vector.scalar_tensor_tensor(nr[:], ar[:], 0.3, ur[:], ALU.add, ALU.subtract)
        nc.vector.tensor_tensor(total, ul[:], ur[:], ALU.add)
        nc.vector.tensor_tensor(drop, ul[:], ur[:], ALU.subtract)
        nc.vector.scalar_tensor_tensor(prc[:], ar[:], 0.01, pr[:], ALU.mult, ALU.max)
        nc.vector.tensor_tensor(nl[:], al[:], ul[:], ALU.subtract)
        nc.vector.tensor_tensor(pl[:], al[:], ul[:], ALU.add)
        nc.vector.scalar_tensor_tensor(nlc[:], al[:], 0.01, nl[:], ALU.mult, ALU.max)
        nc.vector.scalar_tensor_tensor(sr[:], prc[:], 0.01 * 0.3, pl[:], ALU.add, ALU.max)
        nc.vector.tensor_tensor(ns[:], nlc[:], nr[:], ALU.max)

        t, wd, root, rw = face("t"), face("wd"), face("root"), face("rw")
        q1, q2, q3, flux = face("q1"), face("q2"), face("q3"), face("flux")
        nc.vector.scalar_tensor_tensor(t[:], total, -0.5, sr[:], ALU.mult, ALU.add)
        for h in halves:
            nc.vector.tensor_tensor(wd[:, h], sr[:, h], ns[:, h], ALU.add)
            nc.scalar.activation(root[:, h], wd[:, h], ACT.Abs_reciprocal_sqrt)
            nc.scalar.activation(rw[:, h], root[:, h], ACT.Square)
        for h in halves:
            nc.vector.tensor_tensor(q1[:, h], ns[:, h], drop[:, h], ALU.mult)
        for h in halves:
            nc.vector.tensor_tensor(q2[:, h], q1[:, h], t[:, h], ALU.mult)
        for h in halves:
            nc.vector.tensor_tensor(q3[:, h], q2[:, h], rw[:, h], ALU.mult)
        for h, queue in zip(halves, (nc.sync, nc.scalar)):
            nc.vector.tensor_tensor(flux[:, h], q3[:, h], fl[:, h], ALU.add)
            queue.dma_start(out=out[:, h], in_=flux[:, h])
